import numpy as np, ml_dtypes
CORES = [6,14,22,30,38,46,54,62,134,142,150,158,166,174,182,190,262,270,278,286,294,302,310,318,390,398,406,414,422,430,438,446]
N = 32
ROWS, COLS = 4, 8
def setup_inputs(rng):
    return {"x": rng.standard_normal((N, 128, 8), dtype=np.float32).astype(ml_dtypes.bfloat16)}
def reference(x):
    g = x.astype(np.float64).reshape(ROWS, COLS, 128, 8)
    rs = g.sum(axis=1)
    cs = g.sum(axis=0)
    y1 = np.stack([rs[r // COLS] for r in range(N)]).astype(x.dtype)
    y2 = np.stack([cs[r % COLS] for r in range(N)]).astype(x.dtype)
    return {"y1": y1, "y2": y2}

@@ -1,0 +1,74 @@
+from concourse.bass import DstId, RemoteDMATransfer
+from concourse.mybir import AluOpType
+
+COLS = 8
+SCRATCH = {
+    "xs": ("dram", [128, 8], "bfloat16"),
+    "land": ("dram", [COLS, 128, 8], "bfloat16"),
+    "rowsum": ("dram", [128, 8], "bfloat16"),
+    "colx": ("dram", [128, 8], "bfloat16"),
+    "colp": ("dram", [128, 8], "bfloat16"),
+}
+SEMAPHORES = ["ld", "y2i", "sent", "rowin", "rowout", "c1", "c2", "a1", "a2", "st"]
+
+HELPER_CHIP, HELPER_CORE = 0, 2
+
+
+def helper_of(host):
+    return host * 128 + HELPER_CHIP * 8 + HELPER_CORE
+
+
+def dst(topo, d, src):
+    rid, pid = topo.addr(d, src)
+    return DstId(rid=rid, pnc=pid)
+
+
+def rank_program(g, core, T, topo):
+    S = T.sem
+    host = topo.host(core)
+    rank = T.rank_of(core)
+
+    if rank is None:
+        if core != helper_of(host):
+            return
+        row = [T.cores[host * COLS + c] for c in range(COLS)]
+        g.wait_ge(S.rowin, 4 * COLS)
+        g.remote_dma_fused(
+            [RemoteDMATransfer(dst_ids=[dst(topo, d, core) for d in row], dma_engine_mask=0xFF, remote_sem=S.rowout,
+                               srcs=[T.land[c] for c in range(COLS)], dsts=[T.rowsum[:] for d in row], alu_op=1)],
+            local_sem=S.sent)
+        g.wait_ge(S.sent, 8)
+        return
+
+    col = rank % COLS
+    rack_peer = T.cores[(host ^ 1) * COLS + col]
+    cable_peer = T.cores[(3 - host) * COLS + col]
+
+    g.sync.dma_start(T.xs[:], T.x[:]).then_inc(S.ld, 16)
+    g.scalar.dma_start(T.y2[:], T.x[:]).then_inc(S.y2i, 16)
+
+    g.sync.wait_ge(S.rowout, 8)
+    g.sync.dma_start(T.y1[:], T.rowsum[:]).then_inc(S.st, 16)
+
+    g.wait_ge(S.ld, 16)
+    g.remote_dma_fused(
+        [RemoteDMATransfer(dst_ids=[dst(topo, helper_of(host), core)], dma_engine_mask=0x0F, remote_sem=S.rowin,
+                           src=T.xs[:], dst=T.land[col]),
+         RemoteDMATransfer(dst_ids=[dst(topo, rack_peer, core)], dma_engine_mask=0xF0, remote_sem=S.c1,
+                           src=T.xs[:], dst=T.colx[:])],
+        local_sem=S.sent)
+
+    g.wait_ge(S.c1, 4)
+    g.remote_dma_fused(
+        [RemoteDMATransfer(dst_ids=[dst(topo, cable_peer, core)], dma_engine_mask=0xFF, remote_sem=S.c2,
+                           srcs=[T.xs[:], T.colx[:]], dsts=[T.colp[:]], alu_op=1)],
+        local_sem=S.sent)
+
+    g.wait_ge(S.y2i, 16)
+    g.dma_start(T.y2[:], T.colx[:], accum_op=AluOpType.add).then_inc(S.a1, 16)
+    g.wait_ge(S.a1, 16)
+    g.wait_ge(S.c2, 8)
+    g.dma_start(T.y2[:], T.colp[:], accum_op=AluOpType.add).then_inc(S.a2, 16)
+    g.wait_ge(S.a2, 16)
+    g.wait_ge(S.sent, 16)
+    g.wait_ge(S.st, 16)

@@ -2,20 +2,21 @@ from concourse.bass import DstId, RemoteDMATransfer
 from concourse.mybir import AluOpType
 
 COLS = 8
+Q = 4
 SCRATCH = {
-    "xs": ("dram", [128, 8], "bfloat16"),
-    "land": ("dram", [COLS, 128, 8], "bfloat16"),
-    "rowsum": ("dram", [128, 8], "bfloat16"),
-    "colx": ("dram", [128, 8], "bfloat16"),
-    "colp": ("dram", [128, 8], "bfloat16"),
+    "xs": ("dram", [Q, 128, 2], "bfloat16"),
+    "land": ("dram", [COLS, 128, 2], "bfloat16"),
+    "rowsum": ("dram", [Q, 128, 2], "bfloat16"),
+    "colx": ("dram", [Q, 128, 2], "bfloat16"),
+    "colp": ("dram", [Q, 128, 2], "bfloat16"),
 }
 SEMAPHORES = ["ld", "y2i", "sent", "rowin", "rowout", "c1", "c2", "a1", "a2", "st"]
 
-HELPER_CHIP, HELPER_CORE = 0, 2
+HELPER_CORE = 2
 
 
-def helper_of(host):
-    return host * 128 + HELPER_CHIP * 8 + HELPER_CORE
+def helper_of(host, p):
+    return host * 128 + p * 8 + HELPER_CORE
 
 
 def dst(topo, d, src):
@@ -29,15 +30,17 @@ def rank_program(g, core, T, topo):
     rank = T.rank_of(core)
 
     if rank is None:
-        if core != helper_of(host):
+        p = topo.chip(core)
+        if p >= Q or core != helper_of(host, p):
             return
         row = [T.cores[host * COLS + c] for c in range(COLS)]
-        g.wait_ge(S.rowin, 4 * COLS)
+        g.wait_ge(S.rowin, COLS)
         g.remote_dma_fused(
-            [RemoteDMATransfer(dst_ids=[dst(topo, d, core) for d in row], dma_engine_mask=0xFF, remote_sem=S.rowout,
-                               srcs=[T.land[c] for c in range(COLS)], dsts=[T.rowsum[:] for d in row], alu_op=1)],
+            [RemoteDMATransfer(dst_ids=[dst(topo, d, core)], dma_engine_mask=1 << i, remote_sem=S.rowout,
+                               srcs=[T.land[c] for c in range(COLS)], dsts=[T.rowsum[p]], alu_op=1)
+             for i, d in enumerate(row)],
             local_sem=S.sent)
-        g.wait_ge(S.sent, 8)
+        g.wait_ge(S.sent, COLS)
         return
 
     col = rank % COLS
@@ -47,28 +50,28 @@ def rank_program(g, core, T, topo):
     g.sync.dma_start(T.xs[:], T.x[:]).then_inc(S.ld, 16)
     g.scalar.dma_start(T.y2[:], T.x[:]).then_inc(S.y2i, 16)
 
-    g.sync.wait_ge(S.rowout, 8)
+    g.sync.wait_ge(S.rowout, Q)
     g.sync.dma_start(T.y1[:], T.rowsum[:]).then_inc(S.st, 16)
 
     g.wait_ge(S.ld, 16)
     g.remote_dma_fused(
-        [RemoteDMATransfer(dst_ids=[dst(topo, helper_of(host), core)], dma_engine_mask=0x0F, remote_sem=S.rowin,
-                           src=T.xs[:], dst=T.land[col]),
-         RemoteDMATransfer(dst_ids=[dst(topo, rack_peer, core)], dma_engine_mask=0xF0, remote_sem=S.c1,
-                           src=T.xs[:], dst=T.colx[:])],
+        [RemoteDMATransfer(dst_ids=[dst(topo, rack_peer, core)], dma_engine_mask=1 << p, remote_sem=S.c1,
+                           src=T.xs[p], dst=T.colx[p]) for p in range(Q)] +
+        [RemoteDMATransfer(dst_ids=[dst(topo, helper_of(host, p), core)], dma_engine_mask=16 << p, remote_sem=S.rowin,
+                           src=T.xs[p], dst=T.land[col]) for p in range(Q)],
         local_sem=S.sent)
 
-    g.wait_ge(S.c1, 4)
+    g.wait_ge(S.c1, Q)
     g.remote_dma_fused(
-        [RemoteDMATransfer(dst_ids=[dst(topo, cable_peer, core)], dma_engine_mask=0xFF, remote_sem=S.c2,
-                           srcs=[T.xs[:], T.colx[:]], dsts=[T.colp[:]], alu_op=1)],
+        [RemoteDMATransfer(dst_ids=[dst(topo, cable_peer, core)], dma_engine_mask=3 << (2 * p), remote_sem=S.c2,
+                           srcs=[T.xs[p], T.colx[p]], dsts=[T.colp[p]], alu_op=1) for p in range(Q)],
         local_sem=S.sent)
 
     g.wait_ge(S.y2i, 16)
     g.dma_start(T.y2[:], T.colx[:], accum_op=AluOpType.add).then_inc(S.a1, 16)
     g.wait_ge(S.a1, 16)
-    g.wait_ge(S.c2, 8)
+    g.wait_ge(S.c2, 2 * Q)
     g.dma_start(T.y2[:], T.colp[:], accum_op=AluOpType.add).then_inc(S.a2, 16)
     g.wait_ge(S.a2, 16)
-    g.wait_ge(S.sent, 16)
+    g.wait_ge(S.sent, 2 * Q + 2 * Q)
     g.wait_ge(S.st, 16)

from concourse.bass import DstId, RemoteDMATransfer
from concourse.mybir import AluOpType

COLS = 8
Q = 4
SCRATCH = {
    "xs": ("dram", [Q, 128, 2], "bfloat16"),
    "land": ("dram", [COLS, 128, 2], "bfloat16"),
    "rowsum": ("dram", [Q, 128, 2], "bfloat16"),
    "colx": ("dram", [Q, 128, 2], "bfloat16"),
    "colp": ("dram", [Q, 128, 2], "bfloat16"),
}
SEMAPHORES = ["ld", "y2i", "sent", "rowin", "rowout", "c1", "c2", "a1", "a2", "st"]

HELPER_CORE = 2


def helper_of(host, p):
    return host * 128 + p * 8 + HELPER_CORE


def dst(topo, d, src):
    rid, pid = topo.addr(d, src)
    return DstId(rid=rid, pnc=pid)


def rank_program(g, core, T, topo):
    S = T.sem
    host = topo.host(core)
    rank = T.rank_of(core)

    if rank is None:
        p = topo.chip(core)
        if p >= Q or core != helper_of(host, p):
            return
        row = [T.cores[host * COLS + c] for c in range(COLS)]
        g.wait_ge(S.rowin, COLS)
        g.remote_dma_fused(
            [RemoteDMATransfer(dst_ids=[dst(topo, d, core)], dma_engine_mask=1 << i, remote_sem=S.rowout,
                               srcs=[T.land[c] for c in range(COLS)], dsts=[T.rowsum[p]], alu_op=1)
             for i, d in enumerate(row)],
            local_sem=S.sent)
        g.wait_ge(S.sent, COLS)
        return

    col = rank % COLS
    rack_peer = T.cores[(host ^ 1) * COLS + col]
    cable_peer = T.cores[(3 - host) * COLS + col]

    g.sync.dma_start(T.xs[:], T.x[:]).then_inc(S.ld, 16)
    g.scalar.dma_start(T.y2[:], T.x[:]).then_inc(S.y2i, 16)

    g.sync.wait_ge(S.rowout, Q)
    g.sync.dma_start(T.y1[:], T.rowsum[:]).then_inc(S.st, 16)

    g.wait_ge(S.ld, 16)
    g.remote_dma_fused(
        [RemoteDMATransfer(dst_ids=[dst(topo, rack_peer, core)], dma_engine_mask=1 << p, remote_sem=S.c1,
                           src=T.xs[p], dst=T.colx[p]) for p in range(Q)] +
        [RemoteDMATransfer(dst_ids=[dst(topo, helper_of(host, p), core)], dma_engine_mask=16 << p, remote_sem=S.rowin,
                           src=T.xs[p], dst=T.land[col]) for p in range(Q)],
        local_sem=S.sent)

    g.wait_ge(S.c1, Q)
    g.remote_dma_fused(
        [RemoteDMATransfer(dst_ids=[dst(topo, cable_peer, core)], dma_engine_mask=3 << (2 * p), remote_sem=S.c2,
                           srcs=[T.xs[p], T.colx[p]], dsts=[T.colp[p]], alu_op=1) for p in range(Q)],
        local_sem=S.sent)

    g.wait_ge(S.y2i, 16)
    g.dma_start(T.y2[:], T.colx[:], accum_op=AluOpType.add).then_inc(S.a1, 16)
    g.wait_ge(S.a1, 16)
    g.wait_ge(S.c2, 2 * Q)
    g.dma_start(T.y2[:], T.colp[:], accum_op=AluOpType.add).then_inc(S.a2, 16)
    g.wait_ge(S.a2, 16)
    g.wait_ge(S.sent, 2 * Q + 2 * Q)
    g.wait_ge(S.st, 16)
